import numpy as np
import ml_dtypes


def mxq(x, axis, fmt="e4m3"):
    dtype, down = {"e4m3": (ml_dtypes.float8_e4m3fn, 7), "e5m2": (ml_dtypes.float8_e5m2, 14)}[fmt]
    v = np.moveaxis(np.asarray(x, np.float32).astype(ml_dtypes.bfloat16).astype(np.float64), axis, -1)
    blocks = v.reshape(v.shape[:-1] + (-1, 32))
    amax = np.abs(blocks).max(-1, keepdims=True)
    byte = np.maximum(np.where(amax > 0, np.frexp(amax)[1] - 1 + 127, 0) - down, 1)
    scale = np.exp2(byte - 127.0)
    codes = (blocks / scale).astype(np.float32).astype(dtype).astype(np.float64)
    return np.moveaxis((codes * scale).reshape(v.shape), -1, axis)


WIDE = False


def mx_kscale(k):
    if not WIDE:
        return np.ones(k)
    levels = np.array([10, -10, 5, -5, 0])
    if k % 512:
        return np.exp2(np.random.permutation(np.resize(levels, k // 32))).repeat(32)
    a = np.empty((k // 512, 16))
    for p in range(k // 512):
        a[p, :8] = np.random.permutation(np.resize(levels, 8))
        for g in range(8):
            far = levels[np.abs(levels - a[p, g]) >= 10]
            a[p, g + 8] = far[np.random.randint(len(far))]
    return np.exp2(a.ravel()).repeat(32)


def f64(x):
    return np.asarray(x).astype(np.float64)


def striped(idx):
    return np.tile(np.asarray(idx).reshape(-1, 16).T, (8, 1)).astype(np.uint16)


def unstriped(offs):
    return offs[:16].T.reshape(-1).astype(np.int64)


E2M1 = np.array([0.0, 0.5, 1.0, 1.5, 2.0, 3.0, 4.0, 6.0, -0.0, -0.5, -1.0, -1.5, -2.0, -3.0, -4.0, -6.0])


def pack_weight(w, fmt):
    k, n = w.shape
    w = f64(np.asarray(w, np.float32).astype(ml_dtypes.bfloat16)).reshape(k // 32, 32, n)
    amax = np.abs(w).max(1)
    if fmt == "e4m3":
        byte = np.frexp(amax)[1] - 1 + 127 - 7
    else:
        mant, ex = np.frexp(amax / 6.0)
        byte = np.where(mant > 0.5, ex, ex - 1) + 127
    byte = np.clip(np.where(amax > 0, byte, 1), 1, 254)
    scaled = (w * np.exp2(127.0 - byte)[:, None, :]).reshape(k, n).astype(np.float32)
    by_word = np.ascontiguousarray(scaled.reshape(k // 512, 128, 4, n).transpose(0, 1, 3, 2))
    if fmt == "e4m3":
        words = by_word.astype(ml_dtypes.float8_e4m3fn).view(np.uint8)
    else:
        c = by_word.astype(ml_dtypes.float4_e2m1fn).view(np.uint8) & 0xF
        words = (c[..., 0::2] | (c[..., 1::2] << 4)).reshape(k // 512, 128, 2 * n)
    return np.ascontiguousarray(words), np.ascontiguousarray(byte.astype(np.uint8).reshape(k // 512, 16, n))


def unpack_weight(words, scales, fmt):
    g, _, n = scales.shape
    words = np.ascontiguousarray(words).reshape(g, 128, n, -1)
    if fmt == "e4m3":
        vals = words.view(ml_dtypes.float8_e4m3fn).astype(np.float64)
    else:
        nib = np.empty((g, 128, n, 4), np.uint8)
        nib[..., 0::2] = words & 0xF
        nib[..., 1::2] = words >> 4
        vals = E2M1[nib]
    vals = vals * np.repeat(np.exp2(scales.astype(np.float64) - 127.0), 8, axis=1)[..., None]
    return vals.transpose(0, 1, 3, 2).reshape(g * 512, n)


D, T, U, I, J, G = 512, 1024, 1024, 256, 512, 32


def setup_inputs():
    n = np.random.standard_normal
    idx = np.random.permutation(T)[:I]
    idx2 = np.random.permutation(U)[:J]
    fd = mx_kscale(D)
    tabbp = pack_weight(n((D, U)) / fd[:, None], "e4m3")
    return {
        "taba": (n((D, T)) * 1 / np.sqrt(D) * fd[:, None]).astype(np.float32),
        "tabb_words": tabbp[0],
        "tabb_scales": tabbp[1],
        "pw": (np.random.uniform(0.5, 2.0, (1, J))).astype(np.float32),
        "old": (0.3 * n((I, J))).astype(np.float32),
        "offs": striped(idx),
        "offs2": striped(idx2),
    }


def reference(taba, tabb_words, tabb_scales, pw, old, offs, offs2):
    idx = unstriped(offs)
    idx2 = unstriped(offs2)
    tabbu = unpack_weight(tabb_words, tabb_scales, "e4m3")
    tabaidxq = mxq(f64(taba)[:, idx], 0, "e4m3")
    tabbidx2g = tabbu[:, idx2]
    s = tabaidxq.T @ tabbidx2g
    h1 = np.tanh(s)
    m1 = h1.reshape(I, G, J // G).mean(axis=2)
    mr = np.repeat(m1, J // G, axis=1)
    dmr = f64(pw) * (h1 - mr) * 2.0 * (-1.0)
    dm1 = dmr.reshape(I, G, J // G).sum(axis=2)
    e1 = dm1 / 16.0
    r1 = np.repeat(e1, J // G, axis=1)
    dh1 = f64(pw) * (h1 - mr) * 2.0 + r1
    ds = dh1 * (1.0 - np.square(h1))
    y = ds + f64(old)
    return y

@@ -1,0 +1,152 @@
+from contextlib import ExitStack
+
+import concourse.mybir as mybir
+from concourse.masks import make_identity
+
+F32 = mybir.dt.float32
+BF16 = mybir.dt.bfloat16
+I32 = mybir.dt.int32
+U32 = mybir.dt.uint32
+U16 = mybir.dt.uint16
+U8 = mybir.dt.uint8
+FP8X4 = mybir.dt.float8_e4m3fn_x4
+ALU = mybir.AluOpType
+ACT = mybir.ActivationFunctionType
+AX = mybir.AxisListType
+
+D, T, U, I, J = 512, 1024, 1024, 256, 512
+P = 128
+PACK = 4
+GROUP = 16
+ROW_TILES = I // P
+CHUNK = 128
+CHUNKS = J // CHUNK
+FLOPS = 2 * D * I * J
+
+
+def tile_attend_bpairbalance_kernel(tc, taba, tabb_words, tabb_scales, pw, old, offs, offs2, out):
+    nc = tc.nc
+    with ExitStack() as ctx:
+        sb = ctx.enter_context(tc.tile_pool(name="sb", bufs=1))
+        ps = ctx.enter_context(tc.psum_pool(name="ps", bufs=1))
+
+        offs_a = sb.tile([P, I // 16], U16, name="offs_a")
+        offs_b = sb.tile([P, J // 16], U16, name="offs_b")
+
+        b_scale_table = sb.tile([P, U], U8, name="b_scale_table", align_bytes=64)
+        nc.gpsimd.memset(b_scale_table[:].bitcast(I32), 0)
+        scale_rows = tabb_scales[0].bitcast(I32)
+        for q in range(4):
+            nc.scalar.dma_start(b_scale_table[:].bitcast(I32)[32 * q : 32 * q + 4, :], scale_rows[4 * q : 4 * q + 4, :])
+
+        planes = []
+        a_rows = taba.rearrange("(p t) c -> p t c", t=PACK)
+        for t in range(PACK):
+            plane = sb.tile([P, T], F32, name="plane%d" % t)
+            nc.sync.dma_start(plane[:], a_rows[:, t, :])
+            planes.append(plane)
+            if t == 0:
+                nc.sync.dma_start(offs_a[:], offs)
+                nc.sync.dma_start(offs_b[:], offs2)
+
+        b_word_table = sb.tile([P, U], I32, name="b_word_table", align_bytes=64)
+        nc.sync.dma_start(b_word_table[:], tabb_words[0].rearrange("p c r -> p (c r)").bitcast(I32))
+
+        old_sb = sb.tile([P, ROW_TILES, J], F32, name="old_sb")
+        nc.sync.dma_start(old_sb[:], old.rearrange("(h p) j -> p h j", p=P))
+
+        pw_cols = sb.tile([P, PACK], F32, name="pw_cols")
+        nc.scalar.dma_start(pw_cols[:], pw.rearrange("o (p c) -> (o p) c", c=PACK))
+        ident = sb.tile([P, P], F32, name="ident")
+        make_identity(nc, ident[:])
+        pw_ps = ps.tile([P, PACK, P], F32, name="pw_ps")
+        for c in range(PACK):
+            nc.tensor.transpose(pw_ps[:, c, :], pw_cols[:, c : c + 1].to_broadcast([P, P]), ident[:])
+
+        warm = sb.tile([P, 1], F32, name="warm")
+        nc.scalar.activation(warm[:], pw_cols[:, 0:1], ACT.Tanh)
+
+        b_scales = sb.tile([P, J], U8, name="b_scales", align_bytes=64)
+        nc.vector.tensor_copy(b_scales[:], b_scale_table[:].indirect(offs_b[:]))
+
+        grouped = [sb.tile([P, P, PACK], BF16, name="grouped%d" % h, align_bytes=64) for h in range(ROW_TILES)]
+        for t in range(PACK):
+            for h in range(ROW_TILES):
+                nc.vector.tensor_copy(grouped[h][:, :, t], planes[t][:].indirect(offs_a[:, 8 * h : 8 * h + 8]))
+        a_codes, a_scales = [], []
+        for h in range(ROW_TILES):
+            codes = sb.tile([P, P], U32, name="a_codes%d" % h, align_bytes=64)
+            scales = sb.tile([P, P], U8, name="a_scales%d" % h, align_bytes=64)
+            nc.vector.quantize_mx(out=codes[:].bitcast(FP8X4), scales=scales[:], in_=grouped[h][:].rearrange("p i t -> p (i t)"))
+            a_codes.append(codes)
+            a_scales.append(scales)
+
+        hs, sqs = [], []
+        for c in range(CHUNKS):
+            b_codes = sb.tile([P, CHUNK], U32, name="b_codes%d" % c, align_bytes=64)
+            k = CHUNK // 16
+            nc.vector.tensor_copy(b_codes[:], b_word_table[:].bitcast(U32).indirect(offs_b[:, k * c : k * (c + 1)]))
+            s_ps = ps.tile([P, ROW_TILES, CHUNK], F32, name="s_ps%d" % c)
+            for h in range(ROW_TILES):
+                nc.tensor.matmul_mx(
+                    out=s_ps[:, h, :],
+                    lhsT=a_codes[h][:].bitcast(FP8X4),
+                    lhsT_scale=a_scales[h][:],
+                    rhs=b_codes[:].bitcast(FP8X4),
+                    rhs_scale=b_scales[:, c * CHUNK : (c + 1) * CHUNK],
+                    start=True,
+                    stop=True,
+                )
+            hc = sb.tile([P, ROW_TILES * CHUNK], F32, name="h%d" % c)
+            nc.scalar.activation(hc[:], s_ps[:].rearrange("p h j -> p (h j)"), ACT.Tanh)
+            hs.append(hc)
+        for c in range(CHUNKS):
+            sq = sb.tile([P, ROW_TILES * CHUNK], F32, name="sq%d" % c)
+            nc.scalar.activation(sq[:], hs[c][:], ACT.Square)
+            sqs.append(sq)
+
+        W = ROW_TILES * CHUNK
+        NG = W // GROUP
+
+        def by_group(ap):
+            return ap.rearrange("p (g r) -> p g r", r=GROUP)
+
+        def spread(sums):
+            return sums.unsqueeze(2).to_broadcast([P, NG, GROUP])
+
+        def steps(c):
+            s1 = sb.tile([P, NG], F32, name="s1_%d" % c)
+            s2 = sb.tile([P, NG], F32, name="s2_%d" % c)
+            d = sb.tile([P, W], F32, name="d%d" % c)
+            a = sb.tile([P, W], F32, name="a%d" % c)
+            dh = sb.tile([P, W], F32, name="dh%d" % c)
+            ds = sb.tile([P, W], F32, name="ds%d" % c)
+            y = sb.tile([P, ROW_TILES, CHUNK], F32, name="y%d" % c)
+            n = CHUNK // PACK
+            pw_c = pw_ps[:].rearrange("p c m -> p m c")[:, c * n : (c + 1) * n, :].unsqueeze(1).to_broadcast([P, ROW_TILES, n, PACK])
+            cols = slice(c * CHUNK, (c + 1) * CHUNK)
+
+            def last():
+                nc.vector.scalar_tensor_tensor(y[:], ds[:].rearrange("p (h j) -> p h j", h=ROW_TILES), -2.0, old_sb[:, :, cols], ALU.mult, ALU.add)
+                nc.sync.dma_start(out.rearrange("(h p) j -> p h j", p=P)[:, :, cols], y[:])
+
+            return [
+                lambda: nc.vector.tensor_reduce(s1[:], by_group(hs[c][:]), AX.X, ALU.add),
+                lambda: nc.vector.scalar_tensor_tensor(by_group(d[:]), spread(s1[:]), -1.0 / GROUP, by_group(hs[c][:]), ALU.mult, ALU.add),
+                lambda: nc.vector.tensor_tensor(
+                    a[:].rearrange("p (h m c) -> p h m c", h=ROW_TILES, c=PACK),
+                    d[:].rearrange("p (h m c) -> p h m c", h=ROW_TILES, c=PACK),
+                    pw_c,
+                    ALU.mult,
+                ),
+                lambda: nc.vector.tensor_reduce(s2[:], by_group(a[:]), AX.X, ALU.add),
+                lambda: nc.vector.scalar_tensor_tensor(by_group(dh[:]), spread(s2[:]), -1.0 / GROUP, by_group(a[:]), ALU.mult, ALU.add),
+                lambda: nc.vector.scalar_tensor_tensor(ds[:], sqs[c][:], 1.0, dh[:], ALU.subtract, ALU.mult),
+                last,
+            ]
+
+        for c0 in range(0, CHUNKS, 2):
+            first, second = steps(c0), steps(c0 + 1)
+            for f, g in zip(first, second):
+                f()
+                g()

@@ -33,21 +33,23 @@ def tile_attend_bpairbalance_kernel(tc, taba, tabb_words, tabb_scales, pw, old, 
         offs_a = sb.tile([P, I // 16], U16, name="offs_a")
         offs_b = sb.tile([P, J // 16], U16, name="offs_b")
 
+        nc.sync.dma_start(offs_b[:], offs2)
+        nc.sync.dma_start(offs_a[:], offs)
         b_scale_table = sb.tile([P, U], U8, name="b_scale_table", align_bytes=64)
-        nc.gpsimd.memset(b_scale_table[:].bitcast(I32), 0)
         scale_rows = tabb_scales[0].bitcast(I32)
         for q in range(4):
-            nc.scalar.dma_start(b_scale_table[:].bitcast(I32)[32 * q : 32 * q + 4, :], scale_rows[4 * q : 4 * q + 4, :])
+            rows = scale_rows[4 * q : 4 * q + 4, :].unsqueeze(0).to_broadcast([8, 4, U // 4])
+            eng = nc.sync if q < 2 else nc.scalar
+            eng.dma_start(b_scale_table[:].bitcast(I32)[32 * q : 32 * q + 32, :], rows)
 
-        planes = []
         a_rows = taba.rearrange("(p t) c -> p t c", t=PACK)
-        for t in range(PACK):
-            plane = sb.tile([P, T], F32, name="plane%d" % t)
-            nc.sync.dma_start(plane[:], a_rows[:, t, :])
-            planes.append(plane)
-            if t == 0:
-                nc.sync.dma_start(offs_a[:], offs)
-                nc.sync.dma_start(offs_b[:], offs2)
+        early = sb.tile([P, 2, T], F32, name="early")
+        nc.sync.dma_start(early[:], a_rows[:, 0:2, :])
+        planes = {t: sb.tile([P, T], F32, name="plane%d" % t) for t in (2, 3)}
+        nc.sync.dma_start(planes[2][:], a_rows[:, 2, :])
+        pw_cols = sb.tile([P, PACK], F32, name="pw_cols")
+        nc.sync.dma_start(pw_cols[:], pw.rearrange("o (p c) -> (o p) c", c=PACK))
+        nc.sync.dma_start(planes[3][:], a_rows[:, 3, :])
 
         b_word_table = sb.tile([P, U], I32, name="b_word_table", align_bytes=64)
         nc.sync.dma_start(b_word_table[:], tabb_words[0].rearrange("p c r -> p (c r)").bitcast(I32))
@@ -55,8 +57,6 @@ def tile_attend_bpairbalance_kernel(tc, taba, tabb_words, tabb_scales, pw, old, 
         old_sb = sb.tile([P, ROW_TILES, J], F32, name="old_sb")
         nc.sync.dma_start(old_sb[:], old.rearrange("(h p) j -> p h j", p=P))
 
-        pw_cols = sb.tile([P, PACK], F32, name="pw_cols")
-        nc.scalar.dma_start(pw_cols[:], pw.rearrange("o (p c) -> (o p) c", c=PACK))
         ident = sb.tile([P, P], F32, name="ident")
         make_identity(nc, ident[:])
         pw_ps = ps.tile([P, PACK, P], F32, name="pw_ps")
@@ -64,13 +64,18 @@ def tile_attend_bpairbalance_kernel(tc, taba, tabb_words, tabb_scales, pw, old, 
             nc.tensor.transpose(pw_ps[:, c, :], pw_cols[:, c : c + 1].to_broadcast([P, P]), ident[:])
 
         warm = sb.tile([P, 1], F32, name="warm")
-        nc.scalar.activation(warm[:], pw_cols[:, 0:1], ACT.Tanh)
+        nc.scalar.activation(warm[:], ident[:, 0:1], ACT.Tanh)
 
         b_scales = sb.tile([P, J], U8, name="b_scales", align_bytes=64)
         nc.vector.tensor_copy(b_scales[:], b_scale_table[:].indirect(offs_b[:]))
 
         grouped = [sb.tile([P, P, PACK], BF16, name="grouped%d" % h, align_bytes=64) for h in range(ROW_TILES)]
-        for t in range(PACK):
+        picked = sb.tile([P, 2, I], F32, name="picked")
+        for t in range(2):
+            nc.vector.tensor_copy(picked[:, t, :], early[:, t, :].indirect(offs_a[:]))
+        for h in range(ROW_TILES):
+            nc.scalar.copy(grouped[h][:, :, 0:2], picked[:, :, h * P : (h + 1) * P].rearrange("p t i -> p i t"))
+        for t in (2, 3):
             for h in range(ROW_TILES):
                 nc.vector.tensor_copy(grouped[h][:, :, t], planes[t][:].indirect(offs_a[:, 8 * h : 8 * h + 8]))
         a_codes, a_scales = [], []
@@ -100,11 +105,6 @@ def tile_attend_bpairbalance_kernel(tc, taba, tabb_words, tabb_scales, pw, old, 
             hc = sb.tile([P, ROW_TILES * CHUNK], F32, name="h%d" % c)
             nc.scalar.activation(hc[:], s_ps[:].rearrange("p h j -> p (h j)"), ACT.Tanh)
             hs.append(hc)
-        for c in range(CHUNKS):
-            sq = sb.tile([P, ROW_TILES * CHUNK], F32, name="sq%d" % c)
-            nc.scalar.activation(sq[:], hs[c][:], ACT.Square)
-            sqs.append(sq)
-
         W = ROW_TILES * CHUNK
         NG = W // GROUP
 
@@ -114,39 +114,74 @@ def tile_attend_bpairbalance_kernel(tc, taba, tabb_words, tabb_scales, pw, old, 
         def spread(sums):
             return sums.unsqueeze(2).to_broadcast([P, NG, GROUP])
 
-        def steps(c):
-            s1 = sb.tile([P, NG], F32, name="s1_%d" % c)
-            s2 = sb.tile([P, NG], F32, name="s2_%d" % c)
-            d = sb.tile([P, W], F32, name="d%d" % c)
-            a = sb.tile([P, W], F32, name="a%d" % c)
-            dh = sb.tile([P, W], F32, name="dh%d" % c)
-            ds = sb.tile([P, W], F32, name="ds%d" % c)
-            y = sb.tile([P, ROW_TILES, CHUNK], F32, name="y%d" % c)
+        def tiles(name, width):
+            return [sb.tile([P, width], F32, name="%s%d" % (name, c)) for c in range(CHUNKS)]
+
+        s1, s2 = tiles("s1_", NG), tiles("s2_", NG)
+        d, a, dh, ds, y, sq = tiles("d", W), tiles("a", W), tiles("dh", W), tiles("ds", W), tiles("y", W), tiles("sq", W)
+
+        def group_sums(sums, x):
+            nc.vector.tensor_reduce(sums[:], by_group(x[:]), AX.X, ALU.add)
+
+        def centre_v(dst, x, sums):
+            nc.vector.scalar_tensor_tensor(by_group(dst[:]), by_group(x[:]), -float(GROUP), spread(sums[:]), ALU.mult, ALU.add)
+
+        def centre_s(dst, x, sums):
+            for g in range(NG):
+                cols = slice(g * GROUP, (g + 1) * GROUP)
+                nc.scalar.activation(dst[:, cols], x[:, cols], ACT.Identity, bias=sums[:, g : g + 1], scale=-float(GROUP))
+
+        def weigh(c):
             n = CHUNK // PACK
             pw_c = pw_ps[:].rearrange("p c m -> p m c")[:, c * n : (c + 1) * n, :].unsqueeze(1).to_broadcast([P, ROW_TILES, n, PACK])
+            nc.vector.tensor_tensor(
+                a[c][:].rearrange("p (h m c) -> p h m c", h=ROW_TILES, c=PACK),
+                d[c][:].rearrange("p (h m c) -> p h m c", h=ROW_TILES, c=PACK),
+                pw_c,
+                ALU.mult,
+            )
+
+        def square(c):
+            nc.scalar.activation(sq[c][:], hs[c][:], ACT.Square)
+
+        def slope(c):
+            nc.vector.scalar_tensor_tensor(ds[c][:], sq[c][:], 1.0, dh[c][:], ALU.subtract, ALU.mult)
+
+        def finish(c):
             cols = slice(c * CHUNK, (c + 1) * CHUNK)
+            yv = y[c][:].rearrange("p (h j) -> p h j", h=ROW_TILES)
+            nc.vector.scalar_tensor_tensor(yv, ds[c][:].rearrange("p (h j) -> p h j", h=ROW_TILES), -2.0 / (GROUP * GROUP), old_sb[:, :, cols], ALU.mult, ALU.add)
+            nc.sync.dma_start(out.rearrange("(h p) j -> p h j", p=P)[:, :, cols], yv)
 
-            def last():
-                nc.vector.scalar_tensor_tensor(y[:], ds[:].rearrange("p (h j) -> p h j", h=ROW_TILES), -2.0, old_sb[:, :, cols], ALU.mult, ALU.add)
-                nc.sync.dma_start(out.rearrange("(h p) j -> p h j", p=P)[:, :, cols], y[:])
-
-            return [
-                lambda: nc.vector.tensor_reduce(s1[:], by_group(hs[c][:]), AX.X, ALU.add),
-                lambda: nc.vector.scalar_tensor_tensor(by_group(d[:]), spread(s1[:]), -1.0 / GROUP, by_group(hs[c][:]), ALU.mult, ALU.add),
-                lambda: nc.vector.tensor_tensor(
-                    a[:].rearrange("p (h m c) -> p h m c", h=ROW_TILES, c=PACK),
-                    d[:].rearrange("p (h m c) -> p h m c", h=ROW_TILES, c=PACK),
-                    pw_c,
-                    ALU.mult,
-                ),
-                lambda: nc.vector.tensor_reduce(s2[:], by_group(a[:]), AX.X, ALU.add),
-                lambda: nc.vector.scalar_tensor_tensor(by_group(dh[:]), spread(s2[:]), -1.0 / GROUP, by_group(a[:]), ALU.mult, ALU.add),
-                lambda: nc.vector.scalar_tensor_tensor(ds[:], sqs[c][:], 1.0, dh[:], ALU.subtract, ALU.mult),
-                last,
-            ]
-
-        for c0 in range(0, CHUNKS, 2):
-            first, second = steps(c0), steps(c0 + 1)
-            for f, g in zip(first, second):
-                f()
-                g()
+        group_sums(s1[0], hs[0])
+        group_sums(s1[1], hs[1])
+        centre_v(d[0], hs[0], s1[0])
+        group_sums(s1[2], hs[2])
+        centre_s(d[2], hs[2], s1[2])
+        centre_v(d[1], hs[1], s1[1])
+        group_sums(s1[3], hs[3])
+        centre_s(d[3], hs[3], s1[3])
+        weigh(0)
+        weigh(1)
+        group_sums(s2[0], a[0])
+        group_sums(s2[1], a[1])
+        centre_s(dh[0], a[0], s2[0])
+        square(0)
+        centre_s(dh[1], a[1], s2[1])
+        square(1)
+        square(2)
+        square(3)
+        weigh(2)
+        weigh(3)
+        group_sums(s2[2], a[2])
+        group_sums(s2[3], a[3])
+        centre_v(dh[2], a[2], s2[2])
+        slope(0)
+        centre_v(dh[3], a[3], s2[3])
+        finish(0)
+        slope(1)
+        slope(2)
+        finish(1)
+        slope(3)
+        finish(2)
+        finish(3)

@@ -33,21 +33,20 @@ def tile_attend_bpairbalance_kernel(tc, taba, tabb_words, tabb_scales, pw, old, 
         offs_a = sb.tile([P, I // 16], U16, name="offs_a")
         offs_b = sb.tile([P, J // 16], U16, name="offs_b")
 
-        nc.sync.dma_start(offs_b[:], offs2)
-        nc.sync.dma_start(offs_a[:], offs)
         b_scale_table = sb.tile([P, U], U8, name="b_scale_table", align_bytes=64)
-        scale_rows = tabb_scales[0].bitcast(I32)
-        for q in range(4):
-            rows = scale_rows[4 * q : 4 * q + 4, :].unsqueeze(0).to_broadcast([8, 4, U // 4])
-            eng = nc.sync if q < 2 else nc.scalar
-            eng.dma_start(b_scale_table[:].bitcast(I32)[32 * q : 32 * q + 32, :], rows)
-
+        nc.gpsimd.memset(b_scale_table[:].bitcast(I32), 0)
         a_rows = taba.rearrange("(p t) c -> p t c", t=PACK)
-        early = sb.tile([P, 2, T], F32, name="early")
-        nc.sync.dma_start(early[:], a_rows[:, 0:2, :])
-        planes = {t: sb.tile([P, T], F32, name="plane%d" % t) for t in (2, 3)}
-        nc.sync.dma_start(planes[2][:], a_rows[:, 2, :])
+        planes = [sb.tile([P, T], F32, name="plane%d" % t) for t in range(PACK)]
         pw_cols = sb.tile([P, PACK], F32, name="pw_cols")
+        scale_rows = tabb_scales[0].bitcast(I32)
+
+        nc.sync.dma_start(offs_a[:], offs)
+        nc.sync.dma_start(planes[0][:], a_rows[:, 0, :])
+        nc.sync.dma_start(offs_b[:], offs2)
+        for q in range(4):
+            nc.sync.dma_start(b_scale_table[:].bitcast(I32)[32 * q : 32 * q + 4, :], scale_rows[4 * q : 4 * q + 4, :])
+        nc.sync.dma_start(planes[1][:], a_rows[:, 1, :])
+        nc.sync.dma_start(planes[2][:], a_rows[:, 2, :])
         nc.sync.dma_start(pw_cols[:], pw.rearrange("o (p c) -> (o p) c", c=PACK))
         nc.sync.dma_start(planes[3][:], a_rows[:, 3, :])
 
@@ -63,16 +62,13 @@ def tile_attend_bpairbalance_kernel(tc, taba, tabb_words, tabb_scales, pw, old, 
         for c in range(PACK):
             nc.tensor.transpose(pw_ps[:, c, :], pw_cols[:, c : c + 1].to_broadcast([P, P]), ident[:])
 
-        warm = sb.tile([P, 1], F32, name="warm")
-        nc.scalar.activation(warm[:], ident[:, 0:1], ACT.Tanh)
-
         b_scales = sb.tile([P, J], U8, name="b_scales", align_bytes=64)
         nc.vector.tensor_copy(b_scales[:], b_scale_table[:].indirect(offs_b[:]))
 
         grouped = [sb.tile([P, P, PACK], BF16, name="grouped%d" % h, align_bytes=64) for h in range(ROW_TILES)]
         picked = sb.tile([P, 2, I], F32, name="picked")
         for t in range(2):
-            nc.vector.tensor_copy(picked[:, t, :], early[:, t, :].indirect(offs_a[:]))
+            nc.vector.tensor_copy(picked[:, t, :], planes[t][:].indirect(offs_a[:]))
         for h in range(ROW_TILES):
             nc.scalar.copy(grouped[h][:, :, 0:2], picked[:, :, h * P : (h + 1) * P].rearrange("p t i -> p i t"))
         for t in (2, 3):
@@ -147,11 +143,12 @@ def tile_attend_bpairbalance_kernel(tc, taba, tabb_words, tabb_scales, pw, old, 
         def slope(c):
             nc.vector.scalar_tensor_tensor(ds[c][:], sq[c][:], 1.0, dh[c][:], ALU.subtract, ALU.mult)
 
-        def finish(c):
+        def finish(c, tiles_h=slice(0, ROW_TILES)):
             cols = slice(c * CHUNK, (c + 1) * CHUNK)
-            yv = y[c][:].rearrange("p (h j) -> p h j", h=ROW_TILES)
-            nc.vector.scalar_tensor_tensor(yv, ds[c][:].rearrange("p (h j) -> p h j", h=ROW_TILES), -2.0 / (GROUP * GROUP), old_sb[:, :, cols], ALU.mult, ALU.add)
-            nc.sync.dma_start(out.rearrange("(h p) j -> p h j", p=P)[:, :, cols], yv)
+            yv = y[c][:].rearrange("p (h j) -> p h j", h=ROW_TILES)[:, tiles_h, :]
+            dsv = ds[c][:].rearrange("p (h j) -> p h j", h=ROW_TILES)[:, tiles_h, :]
+            nc.vector.scalar_tensor_tensor(yv, dsv, -2.0 / (GROUP * GROUP), old_sb[:, tiles_h, cols], ALU.mult, ALU.add)
+            nc.sync.dma_start(out.rearrange("(h p) j -> p h j", p=P)[:, tiles_h, cols], yv)
 
         group_sums(s1[0], hs[0])
         group_sums(s1[1], hs[1])
@@ -184,4 +181,5 @@ def tile_attend_bpairbalance_kernel(tc, taba, tabb_words, tabb_scales, pw, old, 
         finish(1)
         slope(3)
         finish(2)
-        finish(3)
+        finish(3, slice(0, 1))
+        finish(3, slice(1, 2))

@@ -44,7 +44,7 @@ def tile_attend_bpairbalance_kernel(tc, taba, tabb_words, tabb_scales, pw, old, 
         nc.sync.dma_start(planes[0][:], a_rows[:, 0, :])
         nc.sync.dma_start(offs_b[:], offs2)
         for q in range(4):
-            nc.sync.dma_start(b_scale_table[:].bitcast(I32)[32 * q : 32 * q + 4, :], scale_rows[4 * q : 4 * q + 4, :])
+            (nc.sync if q < 2 else nc.scalar).dma_start(b_scale_table[:].bitcast(I32)[32 * q : 32 * q + 4, :], scale_rows[4 * q : 4 * q + 4, :])
         nc.sync.dma_start(planes[1][:], a_rows[:, 1, :])
         nc.sync.dma_start(planes[2][:], a_rows[:, 2, :])
         nc.sync.dma_start(pw_cols[:], pw.rearrange("o (p c) -> (o p) c", c=PACK))
@@ -152,34 +152,34 @@ def tile_attend_bpairbalance_kernel(tc, taba, tabb_words, tabb_scales, pw, old, 
 
         group_sums(s1[0], hs[0])
         group_sums(s1[1], hs[1])
+        centre_s(d[1], hs[1], s1[1])
         centre_v(d[0], hs[0], s1[0])
         group_sums(s1[2], hs[2])
         centre_s(d[2], hs[2], s1[2])
-        centre_v(d[1], hs[1], s1[1])
-        group_sums(s1[3], hs[3])
-        centre_s(d[3], hs[3], s1[3])
         weigh(0)
-        weigh(1)
+        group_sums(s1[3], hs[3])
         group_sums(s2[0], a[0])
-        group_sums(s2[1], a[1])
         centre_s(dh[0], a[0], s2[0])
         square(0)
+        centre_v(d[3], hs[3], s1[3])
+        weigh(1)
+        weigh(3)
+        group_sums(s2[1], a[1])
         centre_s(dh[1], a[1], s2[1])
         square(1)
-        square(2)
         square(3)
+        square(2)
         weigh(2)
-        weigh(3)
-        group_sums(s2[2], a[2])
         group_sums(s2[3], a[3])
-        centre_v(dh[2], a[2], s2[2])
-        slope(0)
+        group_sums(s2[2], a[2])
         centre_v(dh[3], a[3], s2[3])
+        slope(0)
+        centre_v(dh[2], a[2], s2[2])
         finish(0)
         slope(1)
-        slope(2)
-        finish(1)
         slope(3)
-        finish(2)
-        finish(3, slice(0, 1))
-        finish(3, slice(1, 2))
+        finish(1)
+        slope(2)
+        finish(3)
+        finish(2, slice(0, 1))
+        finish(2, slice(1, 2))

@@ -18,9 +18,13 @@ D, T, U, I, J = 512, 1024, 1024, 256, 512
 P = 128
 PACK = 4
 GROUP = 16
+LIST_ROWS = 16
+QUADRANT = 32
 ROW_TILES = I // P
 CHUNK = 128
 CHUNKS = J // CHUNK
+WIDTH = ROW_TILES * CHUNK
+GROUPS = WIDTH // GROUP
 FLOPS = 2 * D * I * J
 
 
@@ -30,9 +34,8 @@ def tile_attend_bpairbalance_kernel(tc, taba, tabb_words, tabb_scales, pw, old, 
         sb = ctx.enter_context(tc.tile_pool(name="sb", bufs=1))
         ps = ctx.enter_context(tc.psum_pool(name="ps", bufs=1))
 
-        offs_a = sb.tile([P, I // 16], U16, name="offs_a")
-        offs_b = sb.tile([P, J // 16], U16, name="offs_b")
-
+        offs_a = sb.tile([P, I // LIST_ROWS], U16, name="offs_a")
+        offs_b = sb.tile([P, J // LIST_ROWS], U16, name="offs_b")
         b_scale_table = sb.tile([P, U], U8, name="b_scale_table", align_bytes=64)
         nc.gpsimd.memset(b_scale_table[:].bitcast(I32), 0)
         a_rows = taba.rearrange("(p t) c -> p t c", t=PACK)
@@ -43,8 +46,11 @@ def tile_attend_bpairbalance_kernel(tc, taba, tabb_words, tabb_scales, pw, old, 
         nc.sync.dma_start(offs_a[:], offs)
         nc.sync.dma_start(planes[0][:], a_rows[:, 0, :])
         nc.sync.dma_start(offs_b[:], offs2)
-        for q in range(4):
-            (nc.sync if q < 2 else nc.scalar).dma_start(b_scale_table[:].bitcast(I32)[32 * q : 32 * q + 4, :], scale_rows[4 * q : 4 * q + 4, :])
+        for q in range(P // QUADRANT):
+            nc.sync.dma_start(
+                b_scale_table[:].bitcast(I32)[QUADRANT * q : QUADRANT * q + PACK, :],
+                scale_rows[PACK * q : PACK * q + PACK, :],
+            )
         nc.sync.dma_start(planes[1][:], a_rows[:, 1, :])
         nc.sync.dma_start(planes[2][:], a_rows[:, 2, :])
         nc.sync.dma_start(pw_cols[:], pw.rearrange("o (p c) -> (o p) c", c=PACK))
@@ -54,7 +60,7 @@ def tile_attend_bpairbalance_kernel(tc, taba, tabb_words, tabb_scales, pw, old, 
         nc.sync.dma_start(b_word_table[:], tabb_words[0].rearrange("p c r -> p (c r)").bitcast(I32))
 
         old_sb = sb.tile([P, ROW_TILES, J], F32, name="old_sb")
-        nc.sync.dma_start(old_sb[:], old.rearrange("(h p) j -> p h j", p=P))
+        nc.sync.dma_start(old_sb[:], old.rearrange("(r p) j -> p r j", p=P))
 
         ident = sb.tile([P, P], F32, name="ident")
         make_identity(nc, ident[:])
@@ -65,121 +71,131 @@ def tile_attend_bpairbalance_kernel(tc, taba, tabb_words, tabb_scales, pw, old, 
         b_scales = sb.tile([P, J], U8, name="b_scales", align_bytes=64)
         nc.vector.tensor_copy(b_scales[:], b_scale_table[:].indirect(offs_b[:]))
 
-        grouped = [sb.tile([P, P, PACK], BF16, name="grouped%d" % h, align_bytes=64) for h in range(ROW_TILES)]
+        grouped = [sb.tile([P, P, PACK], BF16, name="grouped%d" % r, align_bytes=64) for r in range(ROW_TILES)]
         picked = sb.tile([P, 2, I], F32, name="picked")
-        for t in range(2):
+        for t in (0, 1):
             nc.vector.tensor_copy(picked[:, t, :], planes[t][:].indirect(offs_a[:]))
-        for h in range(ROW_TILES):
-            nc.scalar.copy(grouped[h][:, :, 0:2], picked[:, :, h * P : (h + 1) * P].rearrange("p t i -> p i t"))
+        for r in range(ROW_TILES):
+            nc.scalar.copy(grouped[r][:, :, 0:2], picked[:, :, r * P : (r + 1) * P].rearrange("p t i -> p i t"))
+        tile_cols = P // LIST_ROWS
         for t in (2, 3):
-            for h in range(ROW_TILES):
-                nc.vector.tensor_copy(grouped[h][:, :, t], planes[t][:].indirect(offs_a[:, 8 * h : 8 * h + 8]))
+            for r in range(ROW_TILES):
+                entries = offs_a[:, tile_cols * r : tile_cols * (r + 1)]
+                nc.vector.tensor_copy(grouped[r][:, :, t], planes[t][:].indirect(entries))
         a_codes, a_scales = [], []
-        for h in range(ROW_TILES):
-            codes = sb.tile([P, P], U32, name="a_codes%d" % h, align_bytes=64)
-            scales = sb.tile([P, P], U8, name="a_scales%d" % h, align_bytes=64)
-            nc.vector.quantize_mx(out=codes[:].bitcast(FP8X4), scales=scales[:], in_=grouped[h][:].rearrange("p i t -> p (i t)"))
+        for r in range(ROW_TILES):
+            codes = sb.tile([P, P], U32, name="a_codes%d" % r, align_bytes=64)
+            scales = sb.tile([P, P], U8, name="a_scales%d" % r, align_bytes=64)
+            nc.vector.quantize_mx(
+                out=codes[:].bitcast(FP8X4), scales=scales[:], in_=grouped[r][:].rearrange("p i t -> p (i t)")
+            )
             a_codes.append(codes)
             a_scales.append(scales)
 
-        hs, sqs = [], []
+        chunk_cols = CHUNK // LIST_ROWS
+        h = []
         for c in range(CHUNKS):
             b_codes = sb.tile([P, CHUNK], U32, name="b_codes%d" % c, align_bytes=64)
-            k = CHUNK // 16
-            nc.vector.tensor_copy(b_codes[:], b_word_table[:].bitcast(U32).indirect(offs_b[:, k * c : k * (c + 1)]))
-            s_ps = ps.tile([P, ROW_TILES, CHUNK], F32, name="s_ps%d" % c)
-            for h in range(ROW_TILES):
+            entries = offs_b[:, chunk_cols * c : chunk_cols * (c + 1)]
+            nc.vector.tensor_copy(b_codes[:], b_word_table[:].bitcast(U32).indirect(entries))
+            scores = ps.tile([P, ROW_TILES, CHUNK], F32, name="scores%d" % c)
+            for r in range(ROW_TILES):
                 nc.tensor.matmul_mx(
-                    out=s_ps[:, h, :],
-                    lhsT=a_codes[h][:].bitcast(FP8X4),
-                    lhsT_scale=a_scales[h][:],
+                    out=scores[:, r, :],
+                    lhsT=a_codes[r][:].bitcast(FP8X4),
+                    lhsT_scale=a_scales[r][:],
                     rhs=b_codes[:].bitcast(FP8X4),
                     rhs_scale=b_scales[:, c * CHUNK : (c + 1) * CHUNK],
                     start=True,
                     stop=True,
                 )
-            hc = sb.tile([P, ROW_TILES * CHUNK], F32, name="h%d" % c)
-            nc.scalar.activation(hc[:], s_ps[:].rearrange("p h j -> p (h j)"), ACT.Tanh)
-            hs.append(hc)
-        W = ROW_TILES * CHUNK
-        NG = W // GROUP
+            h_c = sb.tile([P, WIDTH], F32, name="h%d" % c)
+            nc.scalar.activation(h_c[:], scores[:].rearrange("p r j -> p (r j)"), ACT.Tanh)
+            h.append(h_c)
 
-        def by_group(ap):
-            return ap.rearrange("p (g r) -> p g r", r=GROUP)
-
-        def spread(sums):
-            return sums.unsqueeze(2).to_broadcast([P, NG, GROUP])
-
-        def tiles(name, width):
+        def per_chunk(name, width):
             return [sb.tile([P, width], F32, name="%s%d" % (name, c)) for c in range(CHUNKS)]
 
-        s1, s2 = tiles("s1_", NG), tiles("s2_", NG)
-        d, a, dh, ds, y, sq = tiles("d", W), tiles("a", W), tiles("dh", W), tiles("ds", W), tiles("y", W), tiles("sq", W)
+        h_sums, w_sums = per_chunk("h_sums", GROUPS), per_chunk("w_sums", GROUPS)
+        n_h = per_chunk("n_h", WIDTH)
+        w = per_chunk("w", WIDTH)
+        n_w = per_chunk("n_w", WIDTH)
+        slopes = per_chunk("slopes", WIDTH)
+        result = per_chunk("result", WIDTH)
+        squares = per_chunk("squares", WIDTH)
+
+        def by_group(x):
+            return x[:].rearrange("p (g k) -> p g k", k=GROUP)
+
+        def by_row_tile(x):
+            return x[:].rearrange("p (r j) -> p r j", r=ROW_TILES)
 
         def group_sums(sums, x):
-            nc.vector.tensor_reduce(sums[:], by_group(x[:]), AX.X, ALU.add)
+            nc.vector.tensor_reduce(sums[:], by_group(x), AX.X, ALU.add)
 
-        def centre_v(dst, x, sums):
-            nc.vector.scalar_tensor_tensor(by_group(dst[:]), by_group(x[:]), -float(GROUP), spread(sums[:]), ALU.mult, ALU.add)
+        def centre_on_vector(dst, x, sums):
+            spread = sums[:].unsqueeze(2).to_broadcast([P, GROUPS, GROUP])
+            nc.vector.scalar_tensor_tensor(by_group(dst), by_group(x), -float(GROUP), spread, ALU.mult, ALU.add)
 
-        def centre_s(dst, x, sums):
-            for g in range(NG):
+        def centre_on_scalar(dst, x, sums):
+            for g in range(GROUPS):
                 cols = slice(g * GROUP, (g + 1) * GROUP)
                 nc.scalar.activation(dst[:, cols], x[:, cols], ACT.Identity, bias=sums[:, g : g + 1], scale=-float(GROUP))
 
         def weigh(c):
-            n = CHUNK // PACK
-            pw_c = pw_ps[:].rearrange("p c m -> p m c")[:, c * n : (c + 1) * n, :].unsqueeze(1).to_broadcast([P, ROW_TILES, n, PACK])
+            m = CHUNK // PACK
+            pw_chunk = pw_ps[:].rearrange("p c m -> p m c")[:, c * m : (c + 1) * m, :]
             nc.vector.tensor_tensor(
-                a[c][:].rearrange("p (h m c) -> p h m c", h=ROW_TILES, c=PACK),
-                d[c][:].rearrange("p (h m c) -> p h m c", h=ROW_TILES, c=PACK),
-                pw_c,
+                w[c][:].rearrange("p (r m c) -> p r m c", r=ROW_TILES, c=PACK),
+                n_h[c][:].rearrange("p (r m c) -> p r m c", r=ROW_TILES, c=PACK),
+                pw_chunk.unsqueeze(1).to_broadcast([P, ROW_TILES, m, PACK]),
                 ALU.mult,
             )
 
         def square(c):
-            nc.scalar.activation(sq[c][:], hs[c][:], ACT.Square)
+            nc.scalar.activation(squares[c][:], h[c][:], ACT.Square)
 
         def slope(c):
-            nc.vector.scalar_tensor_tensor(ds[c][:], sq[c][:], 1.0, dh[c][:], ALU.subtract, ALU.mult)
+            nc.vector.scalar_tensor_tensor(slopes[c][:], squares[c][:], 1.0, n_w[c][:], ALU.subtract, ALU.mult)
 
-        def finish(c, tiles_h=slice(0, ROW_TILES)):
+        def finish(c, row_tiles):
             cols = slice(c * CHUNK, (c + 1) * CHUNK)
-            yv = y[c][:].rearrange("p (h j) -> p h j", h=ROW_TILES)[:, tiles_h, :]
-            dsv = ds[c][:].rearrange("p (h j) -> p h j", h=ROW_TILES)[:, tiles_h, :]
-            nc.vector.scalar_tensor_tensor(yv, dsv, -2.0 / (GROUP * GROUP), old_sb[:, tiles_h, cols], ALU.mult, ALU.add)
-            nc.sync.dma_start(out.rearrange("(h p) j -> p h j", p=P)[:, tiles_h, cols], yv)
+            y = by_row_tile(result[c])[:, row_tiles, :]
+            factor = -2.0 / (GROUP * GROUP)
+            nc.vector.scalar_tensor_tensor(
+                y, by_row_tile(slopes[c])[:, row_tiles, :], factor, old_sb[:, row_tiles, cols], ALU.mult, ALU.add
+            )
+            nc.sync.dma_start(out.rearrange("(r p) j -> p r j", p=P)[:, row_tiles, cols], y)
 
-        group_sums(s1[0], hs[0])
-        group_sums(s1[1], hs[1])
-        centre_s(d[1], hs[1], s1[1])
-        centre_v(d[0], hs[0], s1[0])
-        group_sums(s1[2], hs[2])
-        centre_s(d[2], hs[2], s1[2])
+        both = slice(0, ROW_TILES)
+        group_sums(h_sums[0], h[0])
+        group_sums(h_sums[1], h[1])
+        centre_on_scalar(n_h[1], h[1], h_sums[1])
+        centre_on_vector(n_h[0], h[0], h_sums[0])
+        group_sums(h_sums[2], h[2])
+        centre_on_scalar(n_h[2], h[2], h_sums[2])
+        for c in range(CHUNKS):
+            square(c)
+        group_sums(h_sums[3], h[3])
         weigh(0)
-        group_sums(s1[3], hs[3])
-        group_sums(s2[0], a[0])
-        centre_s(dh[0], a[0], s2[0])
-        square(0)
-        centre_v(d[3], hs[3], s1[3])
+        centre_on_vector(n_h[3], h[3], h_sums[3])
         weigh(1)
+        group_sums(w_sums[0], w[0])
         weigh(3)
-        group_sums(s2[1], a[1])
-        centre_s(dh[1], a[1], s2[1])
-        square(1)
-        square(3)
-        square(2)
+        group_sums(w_sums[1], w[1])
+        centre_on_scalar(n_w[1], w[1], w_sums[1])
+        centre_on_vector(n_w[0], w[0], w_sums[0])
         weigh(2)
-        group_sums(s2[3], a[3])
-        group_sums(s2[2], a[2])
-        centre_v(dh[3], a[3], s2[3])
+        group_sums(w_sums[3], w[3])
+        centre_on_scalar(n_w[3], w[3], w_sums[3])
         slope(0)
-        centre_v(dh[2], a[2], s2[2])
-        finish(0)
+        group_sums(w_sums[2], w[2])
+        finish(0, both)
         slope(1)
+        centre_on_vector(n_w[2], w[2], w_sums[2])
+        finish(1, both)
         slope(3)
-        finish(1)
         slope(2)
-        finish(3)
-        finish(2, slice(0, 1))
-        finish(2, slice(1, 2))
+        finish(3, both)
+        for r in range(ROW_TILES):
+            finish(2, slice(r, r + 1))

from contextlib import ExitStack

import concourse.mybir as mybir
from concourse.masks import make_identity

F32 = mybir.dt.float32
BF16 = mybir.dt.bfloat16
I32 = mybir.dt.int32
U32 = mybir.dt.uint32
U16 = mybir.dt.uint16
U8 = mybir.dt.uint8
FP8X4 = mybir.dt.float8_e4m3fn_x4
ALU = mybir.AluOpType
ACT = mybir.ActivationFunctionType
AX = mybir.AxisListType

D, T, U, I, J = 512, 1024, 1024, 256, 512
P = 128
PACK = 4
GROUP = 16
LIST_ROWS = 16
QUADRANT = 32
ROW_TILES = I // P
CHUNK = 128
CHUNKS = J // CHUNK
WIDTH = ROW_TILES * CHUNK
GROUPS = WIDTH // GROUP
FLOPS = 2 * D * I * J


def tile_attend_bpairbalance_kernel(tc, taba, tabb_words, tabb_scales, pw, old, offs, offs2, out):
    nc = tc.nc
    with ExitStack() as ctx:
        sb = ctx.enter_context(tc.tile_pool(name="sb", bufs=1))
        ps = ctx.enter_context(tc.psum_pool(name="ps", bufs=1))

        offs_a = sb.tile([P, I // LIST_ROWS], U16, name="offs_a")
        offs_b = sb.tile([P, J // LIST_ROWS], U16, name="offs_b")
        b_scale_table = sb.tile([P, U], U8, name="b_scale_table", align_bytes=64)
        nc.gpsimd.memset(b_scale_table[:].bitcast(I32), 0)
        a_rows = taba.rearrange("(p t) c -> p t c", t=PACK)
        planes = [sb.tile([P, T], F32, name="plane%d" % t) for t in range(PACK)]
        pw_cols = sb.tile([P, PACK], F32, name="pw_cols")
        scale_rows = tabb_scales[0].bitcast(I32)

        nc.sync.dma_start(offs_a[:], offs)
        nc.sync.dma_start(planes[0][:], a_rows[:, 0, :])
        nc.sync.dma_start(offs_b[:], offs2)
        for q in range(P // QUADRANT):
            nc.sync.dma_start(
                b_scale_table[:].bitcast(I32)[QUADRANT * q : QUADRANT * q + PACK, :],
                scale_rows[PACK * q : PACK * q + PACK, :],
            )
        nc.sync.dma_start(planes[1][:], a_rows[:, 1, :])
        nc.sync.dma_start(planes[2][:], a_rows[:, 2, :])
        nc.sync.dma_start(pw_cols[:], pw.rearrange("o (p c) -> (o p) c", c=PACK))
        nc.sync.dma_start(planes[3][:], a_rows[:, 3, :])

        b_word_table = sb.tile([P, U], I32, name="b_word_table", align_bytes=64)
        nc.sync.dma_start(b_word_table[:], tabb_words[0].rearrange("p c r -> p (c r)").bitcast(I32))

        old_sb = sb.tile([P, ROW_TILES, J], F32, name="old_sb")
        nc.sync.dma_start(old_sb[:], old.rearrange("(r p) j -> p r j", p=P))

        ident = sb.tile([P, P], F32, name="ident")
        make_identity(nc, ident[:])
        pw_ps = ps.tile([P, PACK, P], F32, name="pw_ps")
        for c in range(PACK):
            nc.tensor.transpose(pw_ps[:, c, :], pw_cols[:, c : c + 1].to_broadcast([P, P]), ident[:])

        b_scales = sb.tile([P, J], U8, name="b_scales", align_bytes=64)
        nc.vector.tensor_copy(b_scales[:], b_scale_table[:].indirect(offs_b[:]))

        grouped = [sb.tile([P, P, PACK], BF16, name="grouped%d" % r, align_bytes=64) for r in range(ROW_TILES)]
        picked = sb.tile([P, 2, I], F32, name="picked")
        for t in (0, 1):
            nc.vector.tensor_copy(picked[:, t, :], planes[t][:].indirect(offs_a[:]))
        for r in range(ROW_TILES):
            nc.scalar.copy(grouped[r][:, :, 0:2], picked[:, :, r * P : (r + 1) * P].rearrange("p t i -> p i t"))
        tile_cols = P // LIST_ROWS
        for t in (2, 3):
            for r in range(ROW_TILES):
                entries = offs_a[:, tile_cols * r : tile_cols * (r + 1)]
                nc.vector.tensor_copy(grouped[r][:, :, t], planes[t][:].indirect(entries))
        a_codes, a_scales = [], []
        for r in range(ROW_TILES):
            codes = sb.tile([P, P], U32, name="a_codes%d" % r, align_bytes=64)
            scales = sb.tile([P, P], U8, name="a_scales%d" % r, align_bytes=64)
            nc.vector.quantize_mx(
                out=codes[:].bitcast(FP8X4), scales=scales[:], in_=grouped[r][:].rearrange("p i t -> p (i t)")
            )
            a_codes.append(codes)
            a_scales.append(scales)

        chunk_cols = CHUNK // LIST_ROWS
        h = []
        for c in range(CHUNKS):
            b_codes = sb.tile([P, CHUNK], U32, name="b_codes%d" % c, align_bytes=64)
            entries = offs_b[:, chunk_cols * c : chunk_cols * (c + 1)]
            nc.vector.tensor_copy(b_codes[:], b_word_table[:].bitcast(U32).indirect(entries))
            scores = ps.tile([P, ROW_TILES, CHUNK], F32, name="scores%d" % c)
            for r in range(ROW_TILES):
                nc.tensor.matmul_mx(
                    out=scores[:, r, :],
                    lhsT=a_codes[r][:].bitcast(FP8X4),
                    lhsT_scale=a_scales[r][:],
                    rhs=b_codes[:].bitcast(FP8X4),
                    rhs_scale=b_scales[:, c * CHUNK : (c + 1) * CHUNK],
                    start=True,
                    stop=True,
                )
            h_c = sb.tile([P, WIDTH], F32, name="h%d" % c)
            nc.scalar.activation(h_c[:], scores[:].rearrange("p r j -> p (r j)"), ACT.Tanh)
            h.append(h_c)

        def per_chunk(name, width):
            return [sb.tile([P, width], F32, name="%s%d" % (name, c)) for c in range(CHUNKS)]

        h_sums, w_sums = per_chunk("h_sums", GROUPS), per_chunk("w_sums", GROUPS)
        n_h = per_chunk("n_h", WIDTH)
        w = per_chunk("w", WIDTH)
        n_w = per_chunk("n_w", WIDTH)
        slopes = per_chunk("slopes", WIDTH)
        result = per_chunk("result", WIDTH)
        squares = per_chunk("squares", WIDTH)

        def by_group(x):
            return x[:].rearrange("p (g k) -> p g k", k=GROUP)

        def by_row_tile(x):
            return x[:].rearrange("p (r j) -> p r j", r=ROW_TILES)

        def group_sums(sums, x):
            nc.vector.tensor_reduce(sums[:], by_group(x), AX.X, ALU.add)

        def centre_on_vector(dst, x, sums):
            spread = sums[:].unsqueeze(2).to_broadcast([P, GROUPS, GROUP])
            nc.vector.scalar_tensor_tensor(by_group(dst), by_group(x), -float(GROUP), spread, ALU.mult, ALU.add)

        def centre_on_scalar(dst, x, sums):
            for g in range(GROUPS):
                cols = slice(g * GROUP, (g + 1) * GROUP)
                nc.scalar.activation(dst[:, cols], x[:, cols], ACT.Identity, bias=sums[:, g : g + 1], scale=-float(GROUP))

        def weigh(c):
            m = CHUNK // PACK
            pw_chunk = pw_ps[:].rearrange("p c m -> p m c")[:, c * m : (c + 1) * m, :]
            nc.vector.tensor_tensor(
                w[c][:].rearrange("p (r m c) -> p r m c", r=ROW_TILES, c=PACK),
                n_h[c][:].rearrange("p (r m c) -> p r m c", r=ROW_TILES, c=PACK),
                pw_chunk.unsqueeze(1).to_broadcast([P, ROW_TILES, m, PACK]),
                ALU.mult,
            )

        def square(c):
            nc.scalar.activation(squares[c][:], h[c][:], ACT.Square)

        def slope(c):
            nc.vector.scalar_tensor_tensor(slopes[c][:], squares[c][:], 1.0, n_w[c][:], ALU.subtract, ALU.mult)

        def finish(c, row_tiles):
            cols = slice(c * CHUNK, (c + 1) * CHUNK)
            y = by_row_tile(result[c])[:, row_tiles, :]
            factor = -2.0 / (GROUP * GROUP)
            nc.vector.scalar_tensor_tensor(
                y, by_row_tile(slopes[c])[:, row_tiles, :], factor, old_sb[:, row_tiles, cols], ALU.mult, ALU.add
            )
            nc.sync.dma_start(out.rearrange("(r p) j -> p r j", p=P)[:, row_tiles, cols], y)

        both = slice(0, ROW_TILES)
        group_sums(h_sums[0], h[0])
        group_sums(h_sums[1], h[1])
        centre_on_scalar(n_h[1], h[1], h_sums[1])
        centre_on_vector(n_h[0], h[0], h_sums[0])
        group_sums(h_sums[2], h[2])
        centre_on_scalar(n_h[2], h[2], h_sums[2])
        for c in range(CHUNKS):
            square(c)
        group_sums(h_sums[3], h[3])
        weigh(0)
        centre_on_vector(n_h[3], h[3], h_sums[3])
        weigh(1)
        group_sums(w_sums[0], w[0])
        weigh(3)
        group_sums(w_sums[1], w[1])
        centre_on_scalar(n_w[1], w[1], w_sums[1])
        centre_on_vector(n_w[0], w[0], w_sums[0])
        weigh(2)
        group_sums(w_sums[3], w[3])
        centre_on_scalar(n_w[3], w[3], w_sums[3])
        slope(0)
        group_sums(w_sums[2], w[2])
        finish(0, both)
        slope(1)
        centre_on_vector(n_w[2], w[2], w_sums[2])
        finish(1, both)
        slope(3)
        slope(2)
        finish(3, both)
        for r in range(ROW_TILES):
            finish(2, slice(r, r + 1))
